import numpy as np
import ml_dtypes


def mxq(x, axis, fmt="e4m3"):
    dtype, down = {"e4m3": (ml_dtypes.float8_e4m3fn, 7), "e5m2": (ml_dtypes.float8_e5m2, 14)}[fmt]
    v = np.moveaxis(np.asarray(x, np.float32).astype(ml_dtypes.bfloat16).astype(np.float64), axis, -1)
    blocks = v.reshape(v.shape[:-1] + (-1, 32))
    amax = np.abs(blocks).max(-1, keepdims=True)
    byte = np.maximum(np.where(amax > 0, np.frexp(amax)[1] - 1 + 127, 0) - down, 1)
    scale = np.exp2(byte - 127.0)
    codes = (blocks / scale).astype(np.float32).astype(dtype).astype(np.float64)
    return np.moveaxis((codes * scale).reshape(v.shape), -1, axis)


WIDE = False


def mx_kscale(k):
    if not WIDE:
        return np.ones(k)
    levels = np.array([10, -10, 5, -5, 0])
    if k % 512:
        return np.exp2(np.random.permutation(np.resize(levels, k // 32))).repeat(32)
    a = np.empty((k // 512, 16))
    for p in range(k // 512):
        a[p, :8] = np.random.permutation(np.resize(levels, 8))
        for g in range(8):
            far = levels[np.abs(levels - a[p, g]) >= 10]
            a[p, g + 8] = far[np.random.randint(len(far))]
    return np.exp2(a.ravel()).repeat(32)


BF16 = ml_dtypes.bfloat16


def bf(x):
    return np.asarray(x, np.float32).astype(BF16)


def f64(x):
    return np.asarray(x).astype(np.float64)


E2M1 = np.array([0.0, 0.5, 1.0, 1.5, 2.0, 3.0, 4.0, 6.0, -0.0, -0.5, -1.0, -1.5, -2.0, -3.0, -4.0, -6.0])


def pack_weight(w, fmt):
    k, n = w.shape
    w = f64(bf(w)).reshape(k // 32, 32, n)
    amax = np.abs(w).max(1)
    if fmt == "e4m3":
        byte = np.frexp(amax)[1] - 1 + 127 - 7
    else:
        mant, ex = np.frexp(amax / 6.0)
        byte = np.where(mant > 0.5, ex, ex - 1) + 127
    byte = np.clip(np.where(amax > 0, byte, 1), 1, 254)
    scaled = (w * np.exp2(127.0 - byte)[:, None, :]).reshape(k, n).astype(np.float32)
    by_word = np.ascontiguousarray(scaled.reshape(k // 512, 128, 4, n).transpose(0, 1, 3, 2))
    if fmt == "e4m3":
        words = by_word.astype(ml_dtypes.float8_e4m3fn).view(np.uint8)
    else:
        c = by_word.astype(ml_dtypes.float4_e2m1fn).view(np.uint8) & 0xF
        words = c[..., 0::2] | (c[..., 1::2] << 4)
    return np.ascontiguousarray(words), np.ascontiguousarray(byte.astype(np.uint8).reshape(k // 512, 16, n))


def unpack_weight(words, scales, fmt):
    g, p, n, _ = words.shape
    if fmt == "e4m3":
        vals = np.ascontiguousarray(words).view(ml_dtypes.float8_e4m3fn).astype(np.float64)
    else:
        nib = np.empty((g, p, n, 4), np.uint8)
        nib[..., 0::2] = words & 0xF
        nib[..., 1::2] = words >> 4
        vals = E2M1[nib]
    vals = vals * np.repeat(np.exp2(scales.astype(np.float64) - 127.0), 8, axis=1)[..., None]
    return vals.transpose(0, 1, 3, 2).reshape(g * 512, n)
def pack4(w):
    words, scales = pack_weight(w, "e2m1")
    return words.reshape(words.shape[0], 128, -1), scales


def unpack4(words, scales):
    return unpack_weight(words.reshape(words.shape[0], 128, -1, 2), scales, "e2m1")


E4M3FN = np.array([(-1.0 if i & 128 else 1.0) * ((1.0 + (i & 7) / 8.0) * 2.0 ** (((i >> 3) & 15) - 7) if i & 120 else (i & 7) * 2.0 ** -9) for i in range(256)])


def e4m3fn_bytes(y):
    return np.clip(np.asarray(y, np.float64), -448.0, 448.0).astype(np.float32).astype(ml_dtypes.float8_e4m3fn).view(np.uint8)


def e4m3fn_values(b):
    return E4M3FN[b]


N, D, FA, FB = 1024, 1024, 1024, 1024


def _weighted_center(h, t, n):
    mean = np.sum(t[:, None] * h, axis=0)[None, :] / n
    return h - mean


def _weighted_square_sum(c, t):
    return np.sum(t[:, None] * np.square(c), axis=0)


def draw0():
    s, u = mx_kscale(D), mx_kscale(N)
    r = 0.4 + 1.2 * np.random.random_sample(N)
    x = np.random.standard_normal((N, D)) * r[:, None]
    wa = np.random.standard_normal((D, FA)) / np.sqrt(D) * (0.5 + np.random.random_sample(FA))
    wb = np.random.standard_normal((D, FB)) / np.sqrt(D) * (0.5 + np.random.random_sample(FB))
    p = r * (0.8 + 0.4 * np.random.random_sample(N))
    q = 0.5 + np.random.random_sample(N)
    wa_words, wa_scales = pack4(wa / s[:, None])
    wb_words, wb_scales = pack4(wb / s[:, None])
    return {"x": bf(x * s), "wa_words": wa_words, "wa_scales": wa_scales, "wb_words": wb_words, "wb_scales": wb_scales, "p": bf(p * u), "q": bf(q / u)}


def core(x, wa_words, wa_scales, wb_words, wb_scales, p, q):
    p, q = f64(p), f64(q)
    xq = mxq(f64(x), 1, "e4m3")
    ha = np.maximum(xq @ unpack4(wa_words, wa_scales), 0.0)
    hb = np.maximum(xq @ unpack4(wb_words, wb_scales), 0.0)

    t = p * q
    n = np.sum(t)

    ca = _weighted_center(ha, t, n)
    cb = _weighted_center(hb, t, n)

    va = _weighted_square_sum(ca, t)
    vb = _weighted_square_sum(cb, t)

    k = mxq((p[:, None] * ca).T, 1, "e4m3") @ mxq(q[:, None] * cb, 0, "e4m3")

    return 32.0 * k / (np.sqrt(va)[:, None] * np.sqrt(vb)[None, :])


def setup_inputs():
    drawn = draw0()
    full = np.asarray(drawn['x']).astype(np.float64)
    scale = (np.abs(full).reshape(8, 128, 8, 128).max(axis=(1, 3)) / 448.0).astype(np.float32)
    given = {}
    for key, value in drawn.items():
        if key == 'x':
            given['x_bytes'] = e4m3fn_bytes(full / np.repeat(np.repeat(scale.astype(np.float64), 128, axis=0), 128, axis=1))
            given['x_scale'] = scale
        else:
            given[key] = value
    return given


def reference(x_bytes, x_scale, wa_words, wa_scales, wb_words, wb_scales, p, q):
    return core(e4m3fn_values(x_bytes) * np.repeat(np.repeat(x_scale.astype(np.float64), 128, axis=0), 128, axis=1), wa_words, wa_scales, wb_words, wb_scales, p, q)

@@ -1,0 +1,354 @@
+from contextlib import ExitStack
+
+import concourse.mybir as mybir
+from concourse.masks import make_identity
+
+F32 = mybir.dt.float32
+BF16 = mybir.dt.bfloat16
+I32 = mybir.dt.int32
+U32 = mybir.dt.uint32
+U8 = mybir.dt.uint8
+E4M3 = mybir.dt.float8_e4m3fn
+E4M3X4 = mybir.dt.float8_e4m3fn_x4
+E2M1X4 = mybir.dt.float4_e2m1fn_x4
+ALU = mybir.AluOpType
+ACT = mybir.ActivationFunctionType
+AX = mybir.AxisListType
+
+P = 128
+T = 4
+N = 1024
+D = 1024
+F = 1024
+G = N // 512
+KG = D // 512
+NT = G * T
+W = 512
+
+FLOPS = 2 * N * D * 2 * F + 2 * N * F * F
+
+
+def tile_zipitweightedfeaturecorrelation_d2p_kernel(tc, x_bytes, x_scale, wa_words, wa_scales, wb_words, wb_scales, p, q, out):
+    nc = tc.nc
+    with ExitStack() as ctx:
+        keep = ctx.enter_context(tc.tile_pool(name="keep", bufs=1))
+        ring = ctx.enter_context(tc.tile_pool(name="ring", bufs=2))
+        psum = ctx.enter_context(tc.psum_pool(name="psum", bufs=1))
+
+        def bank(i, dtype=F32):
+            return psum.tile([P, 512], dtype, name="bank%d" % i)
+
+        xb = [keep.tile([P, T, D], U8, name="xb%d" % g) for g in range(G)]
+        x_view = x_bytes.rearrange("(g p t) k -> g p t k", p=P, t=T)
+        nc.sync.dma_start(out=xb[0][:, 0:1, :], in_=x_view[0][:, 0:1, :])
+        nc.sync.dma_start(out=xb[0][:, 1:2, :], in_=x_view[0][:, 1:2, :])
+        nc.sync.dma_start(out=xb[0][:, 2:4, :], in_=x_view[0][:, 2:4, :])
+
+        xs = keep.tile([P, G, 8], F32, name="xs")
+        xs_view = x_scale.rearrange("(g s) j -> s g j", g=G)
+        for s in range(4):
+            nc.scalar.dma_start(out=xs[32 * s : 32 * s + 32, :, :], in_=xs_view[s].partition_broadcast(32))
+        p16 = keep.tile([P, G, T], BF16, name="p16")
+        q16 = keep.tile([P, G, T], BF16, name="q16")
+        nc.scalar.dma_start(out=p16[:], in_=p.rearrange("(g p t) -> p g t", p=P, t=T))
+        nc.scalar.dma_start(out=q16[:], in_=q.rearrange("(g p t) -> p g t", p=P, t=T))
+
+        nc.sync.dma_start(out=xb[1][:], in_=x_view[1])
+
+        ident = keep.tile([P, P], F32, name="ident")
+        make_identity(nc, ident[:])
+        ones = keep.tile([P, P], F32, name="ones")
+        nc.gpsimd.memset(ones[:], 1.0)
+
+        words = {}
+        planes = {}
+        for m, w_words in (("b", wb_words), ("a", wa_words)):
+            words[m] = keep.tile([P, KG, 2 * F], U8, name="words_" + m, align_bytes=64)
+            planes[m] = keep.tile([P, KG, F], U8, name="planes_" + m, align_bytes=64)
+        for m, w_scales in (("b", wb_scales), ("a", wa_scales)):
+            nc.gpsimd.memset(planes[m][:].rearrange("p g n -> p (g n)").bitcast(I32), 0)
+            src = w_scales.bitcast(I32).rearrange("g r n -> r g n")
+            for s in range(4):
+                nc.gpsimd.dma_start(out=planes[m][32 * s : 32 * s + 4].bitcast(I32), in_=src[4 * s : 4 * s + 4])
+        for m, w_words, h in (("b", wb_words, 0), ("a", wa_words, 0), ("a", wa_words, 1), ("b", wb_words, 1)):
+            cols = slice(h * 2 * W, (h + 1) * 2 * W)
+            nc.sync.dma_start(
+                out=words[m][:, :, cols].bitcast(I32),
+                in_=w_words[:, :, cols].bitcast(I32).rearrange("g p n -> p g n"),
+            )
+
+        pq = keep.tile([P, 2, NT], F32, name="pq")
+        tw = keep.tile([P, NT], F32, name="tw")
+        rpq = keep.tile([P, 2, NT], F32, name="rpq")
+        rst = keep.tile([P, NT], F32, name="rst")
+        n1 = keep.tile([P, 1], F32, name="n1")
+        rn = keep.tile([P, 1], F32, name="rn")
+        ntn = keep.tile([P, NT], F32, name="ntn")
+
+        def token_weights():
+            nc.vector.tensor_copy(out=pq[:, 0], in_=p16[:].rearrange("p g t -> p (g t)"))
+            nc.vector.tensor_copy(out=pq[:, 1], in_=q16[:].rearrange("p g t -> p (g t)"))
+            nc.vector.tensor_tensor(out=tw[:], in0=pq[:, 0], in1=pq[:, 1], op=ALU.mult)
+            nc.vector.reciprocal(out=rpq[:], in_=pq[:])
+            nc.scalar.activation(out=rst[:], in_=tw[:], func=ACT.Abs_reciprocal_sqrt)
+            nsum = bank(3)
+            nc.tensor.matmul(out=nsum[:, 0:NT], lhsT=ones[:], rhs=tw[:], start=True, stop=True)
+            nc.vector.tensor_reduce(out=n1[:], in_=nsum[:, 0:NT], axis=AX.X, op=ALU.add)
+            nc.vector.reciprocal(out=rn[:], in_=n1[:])
+            nc.vector.tensor_scalar(out=ntn[:], in0=tw[:], scalar1=rn[:], scalar2=-1.0, op0=ALU.mult, op1=ALU.mult)
+
+        groups = [("b", 0), ("a", 0), ("a", 1), ("b", 1)]
+        th = [keep.tile([P, NT, W], F32, name="th%d" % i) for i in range(4)]
+        xcodes = [keep.tile([P, KG * P], U32, name="xcodes%d" % i, align_bytes=64) for i in range(NT)]
+        xplane = [keep.tile([P, KG * P], U8, name="xplane%d" % i, align_bytes=64) for i in range(NT)]
+        codes = [[keep.tile([P, W], U32, name="codes%d_%d" % (i, g), align_bytes=64) for g in range(G)] for i in range(4)]
+        cplane = [[keep.tile([P, W], U8, name="cplane%d_%d" % (i, g), align_bytes=64) for g in range(G)] for i in range(4)]
+        vmean = [keep.tile([P, 4], F32, name="vmean%d" % i) for i in range(4)]
+        var = [keep.tile([P, 4], F32, name="var%d" % i) for i in range(4)]
+        rsd = [keep.tile([P, 4], F32, name="rsd%d" % i) for i in range(4)]
+        rb = keep.tile([P, F], F32, name="rb")
+
+        xw = {}
+        xg = {}
+
+        def widen(i, eng):
+            g, t = divmod(i, T)
+            xw[i] = ring.tile([P, D], BF16, name="xw", bufs=4)
+            for j in range(8):
+                cols = slice(128 * j, 128 * j + 128)
+                src = xb[g][:, t, cols].bitcast(E4M3)
+                if eng == "v":
+                    nc.vector.tensor_scalar(out=xw[i][:, cols], in0=src, scalar1=xs[:, g, j : j + 1], scalar2=None, op0=ALU.mult)
+                else:
+                    nc.scalar.activation(out=xw[i][:, cols], in_=src, func=ACT.Copy, scale=xs[:, g, j : j + 1])
+
+        def x_turn(i, b):
+            bk = bank(b)
+            view = bk[:].rearrange("p (g u r) -> p g u r", g=KG, u=2)
+            wv = xw[i][:].bitcast(F32)
+            for g in range(KG):
+                for u in range(2):
+                    nc.tensor.transpose(view[:, g, u, :], wv[:, 256 * g + u : 256 * (g + 1) : 2], ident[:])
+            xg[i] = ring.tile([P, KG * P * T], BF16, name="xg", bufs=4, align_bytes=64)
+            (nc.vector.tensor_copy if i % 2 else nc.scalar.copy)(
+                out=xg[i][:].bitcast(F32).rearrange("p (g r u) -> p g r u", g=KG, u=2),
+                in_=bk[:].rearrange("p (g u r) -> p g r u", g=KG, u=2),
+            )
+
+        def x_quant(i):
+            nc.vector.quantize_mx(out=xcodes[i][:].bitcast(E4M3X4), scales=xplane[i][:], in_=xg[i][:])
+
+        def stage1(k, i, b):
+            m, h = groups[k]
+            y = bank(b)
+            for g in range(KG):
+                nc.tensor.matmul_mx(
+                    out=y[:],
+                    lhsT=xcodes[i][:, P * g : P * g + P].bitcast(E4M3X4),
+                    lhsT_scale=xplane[i][:, P * g : P * g + P],
+                    rhs=words[m][:, g, 2 * W * h : 2 * W * (h + 1)].bitcast(E2M1X4),
+                    rhs_scale=planes[m][:, g, W * h : W * (h + 1)],
+                    start=(g == 0),
+                    stop=(g == KG - 1),
+                )
+            return y
+
+        def relu(k, i, y, eng="s"):
+            if eng == "s":
+                nc.scalar.activation(out=th[k][:, i, :], in_=y[:], func=ACT.Relu, scale=tw[:, i : i + 1])
+            else:
+                nc.vector.tensor_scalar(out=th[k][:, i, :], in0=y[:], scalar1=tw[:, i : i + 1], scalar2=0.0, op0=ALU.mult, op1=ALU.max)
+
+        def add_turned(z, src, first, last):
+            nc.tensor.matmul(out=z, lhsT=src, rhs=ident[:], start=first, stop=last, is_transpose=True)
+
+        def token_sum(src, z):
+            for fb in range(4):
+                for i in range(NT):
+                    add_turned(z[:, P * fb : P * fb + P], src[:, i, P * fb : P * fb + P], i == 0, i == NT - 1)
+
+        def fold(dst, z):
+            nc.vector.tensor_reduce(out=dst, in_=z[:].rearrange("p (c r) -> p c r", r=P), axis=AX.X, op=ALU.add)
+
+        def spread(vec, b):
+            bk = bank(b)
+            for fb in range(4):
+                nc.tensor.transpose(bk[:, P * fb : P * fb + P], vec[:, fb : fb + 1].to_broadcast([P, P]), ident[:])
+            return bk
+
+        def centre(k, i, sums):
+            nc.vector.scalar_tensor_tensor(
+                out=th[k][:, i, :], in0=sums[:], scalar=ntn[:, i : i + 1], in1=th[k][:, i, :], op0=ALU.mult, op1=ALU.add
+            )
+
+        pc = {}
+
+        def weigh(k, g):
+            m, _ = groups[k]
+            w = 1 if m == "a" else 0
+            pc[k, g] = ring.tile([P, W * T], BF16, name="pc", bufs=4, align_bytes=64)
+            shape = [P, W // 4, T, 4]
+            nc.vector.tensor_tensor(
+                out=pc[k, g][:].rearrange("p (c i t) -> p c t i", i=4, t=T),
+                in0=th[k][:, T * g : T * g + T, :].rearrange("p t (c i) -> p c t i", i=4),
+                in1=rpq[:, w, T * g : T * g + T].unsqueeze(1).unsqueeze(3).to_broadcast(shape),
+                op=ALU.mult,
+            )
+
+        def c_quant(k, g):
+            nc.vector.quantize_mx(out=codes[k][g][:].bitcast(E4M3X4), scales=cplane[k][g][:], in_=pc[k, g][:])
+
+        sq = {}
+
+        def square(k, i):
+            if i == 0:
+                sq[k] = ring.tile([P, NT, W], F32, name="sq", bufs=2)
+            nc.scalar.activation(out=sq[k][:, i, :], in_=th[k][:, i, :], func=ACT.Square, scale=rst[:, i : i + 1])
+
+        def inv_sd(k):
+            m, h = groups[k]
+            nc.scalar.activation(out=rsd[k][:], in_=var[k][:], func=ACT.Abs_reciprocal_sqrt, scale=1.0 / 1024.0 if m == "a" else 1.0)
+
+        def spread_b(k, b):
+            m, h = groups[k]
+            bk = spread(rsd[k], b)
+            nc.scalar.copy(out=rb[:, W * h : W * h + W], in_=bk[:])
+
+        def stage2(ka, fb, kb, b):
+            o = bank(b)
+            cols = slice(P * fb, P * fb + P)
+            for g in range(G):
+                nc.tensor.matmul_mx(
+                    out=o[:],
+                    lhsT=codes[ka][g][:, cols].bitcast(E4M3X4),
+                    lhsT_scale=cplane[ka][g][:, cols],
+                    rhs=codes[kb][g][:].bitcast(E4M3X4),
+                    rhs_scale=cplane[kb][g][:],
+                    start=(g == 0),
+                    stop=(g == G - 1),
+                )
+            return o
+
+        def finish(ka, fb, kb, o):
+            ha, hb = groups[ka][1], groups[kb][1]
+            res = ring.tile([P, W], F32, name="res", bufs=6)
+            nc.vector.scalar_tensor_tensor(
+                out=res[:], in0=o[:], scalar=rsd[ka][:, fb : fb + 1], in1=rb[:, W * hb : W * hb + W], op0=ALU.mult, op1=ALU.mult
+            )
+            r0 = W * ha + P * fb
+            nc.sync.dma_start(out=out[r0 : r0 + P, W * hb : W * hb + W], in_=res[:])
+
+        ctx.enter_context(tc.manual_schedule())
+
+        half = {}
+
+        def pair_add(j):
+            half[j] = ring.tile([P, W], F32, name="half", bufs=4)
+            nc.vector.tensor_tensor(out=half[j][:], in0=th[0][:, 2 * j, :], in1=th[0][:, 2 * j + 1, :], op=ALU.add)
+
+        for s in range(4 + 3):
+            if s < 4:
+                widen(2 * s, "v")
+                widen(2 * s + 1, "s")
+            if s == 0:
+                token_weights()
+            if 0 <= s - 1 < 4:
+                x_turn(2 * s - 2, 4)
+                x_turn(2 * s - 1, 5)
+                x_quant(2 * s - 2)
+                x_quant(2 * s - 1)
+            if 0 <= s - 2 < 4:
+                for i in (2 * s - 4, 2 * s - 3):
+                    relu(0, i, stage1(0, i, 6 + i % 2))
+            if 0 <= s - 3 < 4:
+                pair_add(s - 3)
+        z = bank(0)
+        for fb in range(4):
+            for j in range(4):
+                add_turned(z[:, P * fb : P * fb + P], half[j][:, P * fb : P * fb + P], j == 0, j == 3)
+        YB = [5, 6, 7]
+        n = 0
+        ys = {}
+        for i in range(2):
+            ys[i] = stage1(1, i, YB[n % 3])
+            n += 1
+        fold(vmean[0][:], z)
+        sums = spread(vmean[0], 4)
+        ys[2] = stage1(1, 2, YB[n % 3])
+        n += 1
+
+        SB = [4, 3, 4, 3]
+        for k in range(3):
+            for i in range(NT):
+                relu(k + 1, i, ys.pop(i))
+                if i + 3 < NT:
+                    ys[i + 3] = stage1(k + 1, i + 3, YB[n % 3])
+                    n += 1
+            for i in range(4):
+                centre(k, i, sums)
+            weigh(k, 0)
+            for i in range(4, 8):
+                centre(k, i, sums)
+            z = bank(0)
+            token_sum(th[k + 1], z)
+            if k < 2:
+                for i in range(3):
+                    ys[i] = stage1(k + 2, i, YB[n % 3])
+                    n += 1
+            weigh(k, 1)
+            fold(vmean[k + 1][:], z)
+            sums = spread(vmean[k + 1], SB[k + 1])
+            if k > 0:
+                zv = bank(1)
+                token_sum(sq[k - 1], zv)
+            for i in range(8):
+                square(k, i)
+            c_quant(k, 0)
+            c_quant(k, 1)
+            if k > 0:
+                fold(var[k - 1][:], zv)
+                inv_sd(k - 1)
+                if groups[k - 1][0] == "b":
+                    spread_b(k - 1, 2)
+            if k == 2:
+                held0 = [stage2(1, fb, 0, (1, 2, 5, 6)[fb]) for fb in range(4)]
+        k = 3
+        for i in range(4):
+            centre(k, i, sums)
+            square(k, i)
+        zv = bank(0)
+        token_sum(sq[2], zv)
+        weigh(k, 0)
+        for i in range(4, 8):
+            centre(k, i, sums)
+            square(k, i)
+        weigh(k, 1)
+        fold(var[2][:], zv)
+        inv_sd(2)
+        c_quant(k, 0)
+        finish(1, 0, 0, held0[0])
+        finish(1, 1, 0, held0[1])
+        c_quant(k, 1)
+        zq = [bank(b) for b in (4, 7, 0, 1)]
+        for fb in range(4):
+            for i in range(NT):
+                add_turned(zq[fb][:, 0:P], sq[3][:, i, P * fb : P * fb + P], i == 0, i == NT - 1)
+        finish(1, 2, 0, held0[2])
+        finish(1, 3, 0, held0[3])
+        for fb in range(4):
+            nc.vector.tensor_reduce(out=var[3][:, fb : fb + 1], in_=zq[fb][:, 0:P], axis=AX.X, op=ALU.add)
+        inv_sd(3)
+        for fb in range(4):
+            held0[fb] = stage2(2, fb, 0, (2, 5, 6, 3)[fb])
+        todo = [(ka, fb) for ka in (1, 2) for fb in range(4)]
+        banks = (7, 0, 1, 2, 5, 6, 3, 7)
+        held = {}
+        held[0] = stage2(todo[0][0], todo[0][1], 3, banks[0])
+        held[1] = stage2(todo[1][0], todo[1][1], 3, banks[1])
+        spread_b(3, 4)
+        for fb in range(4):
+            finish(2, fb, 0, held0[fb])
+        for n in range(8):
+            if n + 2 < 8:
+                held[n + 2] = stage2(todo[n + 2][0], todo[n + 2][1], 3, banks[n + 2])
+            finish(todo[n][0], todo[n][1], 3, held[n])

@@ -20,12 +20,62 @@ T = 4
 N = 1024
 D = 1024
 F = 1024
-G = N // 512
-KG = D // 512
+PASS = P * T
+G = N // PASS
+KG = D // PASS
 NT = G * T
+BLOCK = 128
 W = 512
+FB = W // P
+BANKS = 8
+
+GROUPS = (("b", 0), ("a", 0), ("a", W), ("b", W))
+OWN = {"a": 0, "b": 1}
+OUT_SCALE = 32.0
 
 FLOPS = 2 * N * D * 2 * F + 2 * N * F * F
+
+
+def plan(jobs):
+    lag = 180
+    free = {"V": 0.0, "S": 0.0, "P": 0.0, "G": 0.0}
+    kinds = {e: "" for e in free}
+    todo = {e: [j for j in range(len(jobs)) if jobs[j][1] == e] for e in free}
+    ends = {}
+    bank_free = {b: 0.0 for b in range(BANKS)}
+    holds = {}
+    order = []
+    while len(order) < len(jobs):
+        best = None
+        for e in free:
+            ready = []
+            for j in todo[e]:
+                stage, engine, kind, length, after, emit, takes, frees = jobs[j]
+                if any(a not in ends for a in after) or (takes is not None and not bank_free):
+                    continue
+                begin = max([free[e]] + [ends[a] + (lag if jobs[a][1] != e else 0.0) for a in after])
+                if takes is not None:
+                    begin = max(begin, min(bank_free.values()) + lag)
+                ready.append((begin, stage - (0.5 if kind == kinds[e] else 0.0), j))
+            if ready:
+                first = min(ready)[0]
+                pick = min([(s, j) for begin, s, j in ready if begin <= first])[1]
+                if best is None or first < best[0]:
+                    best = (first, pick, e)
+        begin, j, e = best
+        stage, engine, kind, length, after, emit, takes, frees = jobs[j]
+        kinds[e] = kind
+        bank = None
+        if takes is not None:
+            bank = min(bank_free, key=lambda b: bank_free[b])
+            holds[takes] = bank
+            bank_free.pop(bank)
+        ends[j] = free[e] = begin + length
+        if frees is not None:
+            bank_free[holds[frees]] = ends[j]
+        todo[e].remove(j)
+        order.append((j, bank))
+    return order
 
 
 def tile_zipitweightedfeaturecorrelation_d2p_kernel(tc, x_bytes, x_scale, wa_words, wa_scales, wb_words, wb_scales, p, q, out):
@@ -35,320 +85,343 @@ def tile_zipitweightedfeaturecorrelation_d2p_kernel(tc, x_bytes, x_scale, wa_wor
         ring = ctx.enter_context(tc.tile_pool(name="ring", bufs=2))
         psum = ctx.enter_context(tc.psum_pool(name="psum", bufs=1))
 
-        def bank(i, dtype=F32):
-            return psum.tile([P, 512], dtype, name="bank%d" % i)
+        xs_all = keep.tile([P, (N // BLOCK) * (D // BLOCK)], F32, name="xs_all")
+        nc.scalar.dma_start(out=xs_all[:], in_=x_scale.rearrange("i j -> (i j)").partition_broadcast(P))
+        weight16 = []
+        for name, src in (("p16", p), ("q16", q)):
+            weight16.append(keep.tile([P, G, T], BF16, name=name))
+            nc.scalar.dma_start(out=weight16[-1][:], in_=src.rearrange("(g p t) -> p g t", p=P, t=T))
 
-        xb = [keep.tile([P, T, D], U8, name="xb%d" % g) for g in range(G)]
         x_view = x_bytes.rearrange("(g p t) k -> g p t k", p=P, t=T)
-        nc.sync.dma_start(out=xb[0][:, 0:1, :], in_=x_view[0][:, 0:1, :])
-        nc.sync.dma_start(out=xb[0][:, 1:2, :], in_=x_view[0][:, 1:2, :])
-        nc.sync.dma_start(out=xb[0][:, 2:4, :], in_=x_view[0][:, 2:4, :])
-
-        xs = keep.tile([P, G, 8], F32, name="xs")
-        xs_view = x_scale.rearrange("(g s) j -> s g j", g=G)
-        for s in range(4):
-            nc.scalar.dma_start(out=xs[32 * s : 32 * s + 32, :, :], in_=xs_view[s].partition_broadcast(32))
-        p16 = keep.tile([P, G, T], BF16, name="p16")
-        q16 = keep.tile([P, G, T], BF16, name="q16")
-        nc.scalar.dma_start(out=p16[:], in_=p.rearrange("(g p t) -> p g t", p=P, t=T))
-        nc.scalar.dma_start(out=q16[:], in_=q.rearrange("(g p t) -> p g t", p=P, t=T))
-
-        nc.sync.dma_start(out=xb[1][:], in_=x_view[1])
+        xb = [keep.tile([P, T, D], U8, name="xb%d" % g) for g in range(G)]
+        for g, t0, t1 in ((0, 0, 1), (0, 1, 2), (0, 2, 4), (1, 0, 4)):
+            nc.sync.dma_start(out=xb[g][:, t0:t1, :], in_=x_view[g][:, t0:t1, :])
 
         ident = keep.tile([P, P], F32, name="ident")
         make_identity(nc, ident[:])
         ones = keep.tile([P, P], F32, name="ones")
         nc.gpsimd.memset(ones[:], 1.0)
 
-        words = {}
-        planes = {}
-        for m, w_words in (("b", wb_words), ("a", wa_words)):
+        words, planes = {}, {}
+        for m, w_scales in (("b", wb_scales), ("a", wa_scales)):
             words[m] = keep.tile([P, KG, 2 * F], U8, name="words_" + m, align_bytes=64)
             planes[m] = keep.tile([P, KG, F], U8, name="planes_" + m, align_bytes=64)
-        for m, w_scales in (("b", wb_scales), ("a", wa_scales)):
             nc.gpsimd.memset(planes[m][:].rearrange("p g n -> p (g n)").bitcast(I32), 0)
             src = w_scales.bitcast(I32).rearrange("g r n -> r g n")
-            for s in range(4):
-                nc.gpsimd.dma_start(out=planes[m][32 * s : 32 * s + 4].bitcast(I32), in_=src[4 * s : 4 * s + 4])
-        for m, w_words, h in (("b", wb_words, 0), ("a", wa_words, 0), ("a", wa_words, 1), ("b", wb_words, 1)):
-            cols = slice(h * 2 * W, (h + 1) * 2 * W)
-            nc.sync.dma_start(
-                out=words[m][:, :, cols].bitcast(I32),
-                in_=w_words[:, :, cols].bitcast(I32).rearrange("g p n -> p g n"),
-            )
+            for r in range(4):
+                nc.gpsimd.dma_start(out=planes[m][32 * r : 32 * r + 4].bitcast(I32), in_=src[4 * r : 4 * r + 4])
+        for m, c0 in GROUPS:
+            cols = slice(2 * c0, 2 * (c0 + W))
+            w_words = wa_words if m == "a" else wb_words
+            nc.sync.dma_start(out=words[m][:, :, cols].bitcast(I32), in_=w_words[:, :, cols].bitcast(I32).rearrange("g p n -> p g n"))
+
+        xs = keep.tile([P, G, D // BLOCK], F32, name="xs")
+        for r in range(4):
+            rows = slice(32 * r, 32 * r + 32)
+            nc.vector.tensor_copy(out=xs[rows], in_=xs_all[rows].rearrange("p (g r j) -> p r g j", g=G, r=4)[:, r])
 
         pq = keep.tile([P, 2, NT], F32, name="pq")
-        tw = keep.tile([P, NT], F32, name="tw")
         rpq = keep.tile([P, 2, NT], F32, name="rpq")
+        tw = keep.tile([P, NT], F32, name="tw")
         rst = keep.tile([P, NT], F32, name="rst")
-        n1 = keep.tile([P, 1], F32, name="n1")
-        rn = keep.tile([P, 1], F32, name="rn")
         ntn = keep.tile([P, NT], F32, name="ntn")
+        n_sum = keep.tile([P, 1], F32, name="n_sum")
+        rn = keep.tile([P, 1], F32, name="rn")
+        th = [keep.tile([P, NT, W], F32, name="th%d" % u) for u in range(len(GROUPS))]
+        x_codes = [keep.tile([P, KG * P], U32, name="x_codes%d" % i, align_bytes=64) for i in range(NT)]
+        x_plane = [keep.tile([P, KG * P], U8, name="x_plane%d" % i, align_bytes=64) for i in range(NT)]
+        c_codes = [[keep.tile([P, W], U32, name="c_codes%d_%d" % (u, g), align_bytes=64) for g in range(G)] for u in range(len(GROUPS))]
+        c_plane = [[keep.tile([P, W], U8, name="c_plane%d_%d" % (u, g), align_bytes=64) for g in range(G)] for u in range(len(GROUPS))]
+        sums = [keep.tile([P, FB], F32, name="sums%d" % u) for u in range(len(GROUPS))]
+        var = [keep.tile([P, FB], F32, name="var%d" % u) for u in range(len(GROUPS))]
+        rsd = [keep.tile([P, FB], F32, name="rsd%d" % u) for u in range(len(GROUPS))]
+        rb = {u: keep.tile([P, W], F32, name="rb%d" % u) for u in range(len(GROUPS)) if GROUPS[u][0] == "b"}
 
-        def token_weights():
-            nc.vector.tensor_copy(out=pq[:, 0], in_=p16[:].rearrange("p g t -> p (g t)"))
-            nc.vector.tensor_copy(out=pq[:, 1], in_=q16[:].rearrange("p g t -> p (g t)"))
+        held = {}
+        xw, xg, pc, sq, mid = {}, {}, {}, {}, {}
+
+        def turn(dst, src, first=True, last=True):
+            nc.tensor.matmul(out=dst, lhsT=src, rhs=ident[:], start=first, stop=last, is_transpose=True)
+
+        def add_up(bank, cols, tiles, at_start=True, at_end=True):
+            for i, tile in enumerate(tiles):
+                turn(bank[:, cols], tile, at_start and i == 0, at_end and i == len(tiles) - 1)
+
+        def fold(dst, bank, width):
+            nc.vector.tensor_reduce(out=dst, in_=bank[:, 0:width].rearrange("p (c r) -> p c r", r=P), axis=AX.X, op=ALU.add)
+
+        def spread(bank, vec):
+            for fb in range(FB):
+                turn(bank[:, P * fb : P * fb + P], vec[:, fb : fb + 1].to_broadcast([P, P]))
+
+        def weights():
+            for own in range(2):
+                nc.vector.tensor_copy(out=pq[:, own], in_=weight16[own][:].rearrange("p g t -> p (g t)"))
             nc.vector.tensor_tensor(out=tw[:], in0=pq[:, 0], in1=pq[:, 1], op=ALU.mult)
             nc.vector.reciprocal(out=rpq[:], in_=pq[:])
             nc.scalar.activation(out=rst[:], in_=tw[:], func=ACT.Abs_reciprocal_sqrt)
-            nsum = bank(3)
-            nc.tensor.matmul(out=nsum[:, 0:NT], lhsT=ones[:], rhs=tw[:], start=True, stop=True)
-            nc.vector.tensor_reduce(out=n1[:], in_=nsum[:, 0:NT], axis=AX.X, op=ALU.add)
-            nc.vector.reciprocal(out=rn[:], in_=n1[:])
+
+        def count(bank):
+            held["n"] = bank
+            nc.tensor.matmul(out=bank[:, 0:NT], lhsT=ones[:], rhs=tw[:], start=True, stop=True)
+
+        def count_scale():
+            nc.vector.tensor_reduce(out=n_sum[:], in_=held["n"][:, 0:NT], axis=AX.X, op=ALU.add)
+            nc.vector.reciprocal(out=rn[:], in_=n_sum[:])
             nc.vector.tensor_scalar(out=ntn[:], in0=tw[:], scalar1=rn[:], scalar2=-1.0, op0=ALU.mult, op1=ALU.mult)
 
-        groups = [("b", 0), ("a", 0), ("a", 1), ("b", 1)]
-        th = [keep.tile([P, NT, W], F32, name="th%d" % i) for i in range(4)]
-        xcodes = [keep.tile([P, KG * P], U32, name="xcodes%d" % i, align_bytes=64) for i in range(NT)]
-        xplane = [keep.tile([P, KG * P], U8, name="xplane%d" % i, align_bytes=64) for i in range(NT)]
-        codes = [[keep.tile([P, W], U32, name="codes%d_%d" % (i, g), align_bytes=64) for g in range(G)] for i in range(4)]
-        cplane = [[keep.tile([P, W], U8, name="cplane%d_%d" % (i, g), align_bytes=64) for g in range(G)] for i in range(4)]
-        vmean = [keep.tile([P, 4], F32, name="vmean%d" % i) for i in range(4)]
-        var = [keep.tile([P, 4], F32, name="var%d" % i) for i in range(4)]
-        rsd = [keep.tile([P, 4], F32, name="rsd%d" % i) for i in range(4)]
-        rb = keep.tile([P, F], F32, name="rb")
-
-        xw = {}
-        xg = {}
-
-        def widen(i, eng):
+        def widen(i, on_vector):
             g, t = divmod(i, T)
-            xw[i] = ring.tile([P, D], BF16, name="xw", bufs=4)
-            for j in range(8):
-                cols = slice(128 * j, 128 * j + 128)
-                src = xb[g][:, t, cols].bitcast(E4M3)
-                if eng == "v":
-                    nc.vector.tensor_scalar(out=xw[i][:, cols], in0=src, scalar1=xs[:, g, j : j + 1], scalar2=None, op0=ALU.mult)
+            xw[i] = ring.tile([P, D], BF16, name="xw", bufs=6)
+            for j in range(D // BLOCK):
+                cols = slice(BLOCK * j, BLOCK * (j + 1))
+                src, scale = xb[g][:, t, cols].bitcast(E4M3), xs[:, g, j : j + 1]
+                if on_vector:
+                    nc.vector.tensor_scalar(out=xw[i][:, cols], in0=src, scalar1=scale, scalar2=None, op0=ALU.mult)
                 else:
-                    nc.scalar.activation(out=xw[i][:, cols], in_=src, func=ACT.Copy, scale=xs[:, g, j : j + 1])
+                    nc.scalar.activation(out=xw[i][:, cols], in_=src, func=ACT.Copy, scale=scale)
 
-        def x_turn(i, b):
-            bk = bank(b)
-            view = bk[:].rearrange("p (g u r) -> p g u r", g=KG, u=2)
-            wv = xw[i][:].bitcast(F32)
+        def turn_x(i, bank):
+            held["x", i] = bank
+            pairs = xw[i][:].bitcast(F32)
             for g in range(KG):
-                for u in range(2):
-                    nc.tensor.transpose(view[:, g, u, :], wv[:, 256 * g + u : 256 * (g + 1) : 2], ident[:])
-            xg[i] = ring.tile([P, KG * P * T], BF16, name="xg", bufs=4, align_bytes=64)
-            (nc.vector.tensor_copy if i % 2 else nc.scalar.copy)(
-                out=xg[i][:].bitcast(F32).rearrange("p (g r u) -> p g r u", g=KG, u=2),
-                in_=bk[:].rearrange("p (g u r) -> p g r u", g=KG, u=2),
+                for v in range(2):
+                    turn(bank[:, P * (2 * g + v) : P * (2 * g + v + 1)], pairs[:, 256 * g + v : 256 * (g + 1) : 2])
+
+        def lift_x(i):
+            xg[i] = ring.tile([P, KG * P * T], BF16, name="xg", bufs=6, align_bytes=64)
+            nc.scalar.copy(
+                out=xg[i][:].bitcast(F32).rearrange("p (g r v) -> p g r v", g=KG, v=2),
+                in_=held["x", i][:].rearrange("p (g v r) -> p g r v", g=KG, v=2),
             )
 
-        def x_quant(i):
-            nc.vector.quantize_mx(out=xcodes[i][:].bitcast(E4M3X4), scales=xplane[i][:], in_=xg[i][:])
+        def quantise_x(i):
+            nc.vector.quantize_mx(out=x_codes[i][:].bitcast(E4M3X4), scales=x_plane[i][:], in_=xg[i][:])
 
-        def stage1(k, i, b):
-            m, h = groups[k]
-            y = bank(b)
+        def multiply_x(u, i, bank):
+            held["y", u, i] = bank
+            m, c0 = GROUPS[u]
             for g in range(KG):
                 nc.tensor.matmul_mx(
-                    out=y[:],
-                    lhsT=xcodes[i][:, P * g : P * g + P].bitcast(E4M3X4),
-                    lhsT_scale=xplane[i][:, P * g : P * g + P],
-                    rhs=words[m][:, g, 2 * W * h : 2 * W * (h + 1)].bitcast(E2M1X4),
-                    rhs_scale=planes[m][:, g, W * h : W * (h + 1)],
+                    out=bank[:],
+                    lhsT=x_codes[i][:, P * g : P * g + P].bitcast(E4M3X4),
+                    lhsT_scale=x_plane[i][:, P * g : P * g + P],
+                    rhs=words[m][:, g, 2 * c0 : 2 * (c0 + W)].bitcast(E2M1X4),
+                    rhs_scale=planes[m][:, g, c0 : c0 + W],
                     start=(g == 0),
                     stop=(g == KG - 1),
                 )
-            return y
 
-        def relu(k, i, y, eng="s"):
-            if eng == "s":
-                nc.scalar.activation(out=th[k][:, i, :], in_=y[:], func=ACT.Relu, scale=tw[:, i : i + 1])
+        def relu(u, i, on_vector):
+            y, t = held["y", u, i], tw[:, i : i + 1]
+            if on_vector:
+                nc.vector.tensor_scalar(out=th[u][:, i, :], in0=y[:], scalar1=t, scalar2=0.0, op0=ALU.mult, op1=ALU.max)
             else:
-                nc.vector.tensor_scalar(out=th[k][:, i, :], in0=y[:], scalar1=tw[:, i : i + 1], scalar2=0.0, op0=ALU.mult, op1=ALU.max)
+                nc.scalar.activation(out=th[u][:, i, :], in_=y[:], func=ACT.Relu, scale=t)
 
-        def add_turned(z, src, first, last):
-            nc.tensor.matmul(out=z, lhsT=src, rhs=ident[:], start=first, stop=last, is_transpose=True)
-
-        def token_sum(src, z):
-            for fb in range(4):
-                for i in range(NT):
-                    add_turned(z[:, P * fb : P * fb + P], src[:, i, P * fb : P * fb + P], i == 0, i == NT - 1)
-
-        def fold(dst, z):
-            nc.vector.tensor_reduce(out=dst, in_=z[:].rearrange("p (c r) -> p c r", r=P), axis=AX.X, op=ALU.add)
-
-        def spread(vec, b):
-            bk = bank(b)
-            for fb in range(4):
-                nc.tensor.transpose(bk[:, P * fb : P * fb + P], vec[:, fb : fb + 1].to_broadcast([P, P]), ident[:])
-            return bk
-
-        def centre(k, i, sums):
+        def centre(u, i):
             nc.vector.scalar_tensor_tensor(
-                out=th[k][:, i, :], in0=sums[:], scalar=ntn[:, i : i + 1], in1=th[k][:, i, :], op0=ALU.mult, op1=ALU.add
+                out=th[u][:, i, :], in0=held["mean", u][:], scalar=ntn[:, i : i + 1], in1=th[u][:, i, :], op0=ALU.mult, op1=ALU.add
             )
 
-        pc = {}
-
-        def weigh(k, g):
-            m, _ = groups[k]
-            w = 1 if m == "a" else 0
-            pc[k, g] = ring.tile([P, W * T], BF16, name="pc", bufs=4, align_bytes=64)
-            shape = [P, W // 4, T, 4]
+        def weigh(u, g):
+            other = 1 - OWN[GROUPS[u][0]]
+            pc[u, g] = ring.tile([P, W * T], BF16, name="pc", bufs=4, align_bytes=64)
             nc.vector.tensor_tensor(
-                out=pc[k, g][:].rearrange("p (c i t) -> p c t i", i=4, t=T),
-                in0=th[k][:, T * g : T * g + T, :].rearrange("p t (c i) -> p c t i", i=4),
-                in1=rpq[:, w, T * g : T * g + T].unsqueeze(1).unsqueeze(3).to_broadcast(shape),
+                out=pc[u, g][:].rearrange("p (c i t) -> p c t i", i=4, t=T),
+                in0=th[u][:, T * g : T * g + T, :].rearrange("p t (c i) -> p c t i", i=4),
+                in1=rpq[:, other, T * g : T * g + T].unsqueeze(1).unsqueeze(3).to_broadcast([P, W // 4, T, 4]),
                 op=ALU.mult,
             )
 
-        def c_quant(k, g):
-            nc.vector.quantize_mx(out=codes[k][g][:].bitcast(E4M3X4), scales=cplane[k][g][:], in_=pc[k, g][:])
+        def quantise_c(u, g):
+            nc.vector.quantize_mx(out=c_codes[u][g][:].bitcast(E4M3X4), scales=c_plane[u][g][:], in_=pc[u, g][:])
 
-        sq = {}
-
-        def square(k, i):
+        def square(u, i):
             if i == 0:
-                sq[k] = ring.tile([P, NT, W], F32, name="sq", bufs=2)
-            nc.scalar.activation(out=sq[k][:, i, :], in_=th[k][:, i, :], func=ACT.Square, scale=rst[:, i : i + 1])
+                sq[u] = ring.tile([P, NT, W], F32, name="sq", bufs=2)
+            nc.scalar.activation(out=sq[u][:, i, :], in_=th[u][:, i, :], func=ACT.Square, scale=rst[:, i : i + 1])
 
-        def inv_sd(k):
-            m, h = groups[k]
-            nc.scalar.activation(out=rsd[k][:], in_=var[k][:], func=ACT.Abs_reciprocal_sqrt, scale=1.0 / 1024.0 if m == "a" else 1.0)
+        def fold_squares(u):
+            scrap = ring.tile([P, W], F32, name="scrap", bufs=2)
+            for fb in range(FB):
+                cols = slice(P * fb, P * fb + P)
+                nc.scalar.activation(out=scrap[:, cols], in_=held["var", u][:, cols], func=ACT.Copy, accum_out=var[u][:, fb : fb + 1])
 
-        def spread_b(k, b):
-            m, h = groups[k]
-            bk = spread(rsd[k], b)
-            nc.scalar.copy(out=rb[:, W * h : W * h + W], in_=bk[:])
+        def root(u):
+            unit = 1.0 / OUT_SCALE**2 if GROUPS[u][0] == "a" else 1.0
+            nc.scalar.activation(out=rsd[u][:], in_=var[u][:], func=ACT.Abs_reciprocal_sqrt, scale=unit)
 
-        def stage2(ka, fb, kb, b):
-            o = bank(b)
+        def multiply_c(ua, fb, ub, bank):
+            held["out", ua, fb, ub] = bank
             cols = slice(P * fb, P * fb + P)
             for g in range(G):
                 nc.tensor.matmul_mx(
-                    out=o[:],
-                    lhsT=codes[ka][g][:, cols].bitcast(E4M3X4),
-                    lhsT_scale=cplane[ka][g][:, cols],
-                    rhs=codes[kb][g][:].bitcast(E4M3X4),
-                    rhs_scale=cplane[kb][g][:],
+                    out=bank[:],
+                    lhsT=c_codes[ua][g][:, cols].bitcast(E4M3X4),
+                    lhsT_scale=c_plane[ua][g][:, cols],
+                    rhs=c_codes[ub][g][:].bitcast(E4M3X4),
+                    rhs_scale=c_plane[ub][g][:],
                     start=(g == 0),
                     stop=(g == G - 1),
                 )
-            return o
 
-        def finish(ka, fb, kb, o):
-            ha, hb = groups[ka][1], groups[kb][1]
+        def store(ua, fb, ub, tile):
+            r0, c0 = GROUPS[ua][1] + P * fb, GROUPS[ub][1]
+            nc.sync.dma_start(out=out[r0 : r0 + P, c0 : c0 + W], in_=tile[:])
+
+        def finish(ua, fb, ub):
             res = ring.tile([P, W], F32, name="res", bufs=6)
             nc.vector.scalar_tensor_tensor(
-                out=res[:], in0=o[:], scalar=rsd[ka][:, fb : fb + 1], in1=rb[:, W * hb : W * hb + W], op0=ALU.mult, op1=ALU.mult
+                out=res[:], in0=held["out", ua, fb, ub][:], scalar=rsd[ua][:, fb : fb + 1], in1=rb[ub][:], op0=ALU.mult, op1=ALU.mult
             )
-            r0 = W * ha + P * fb
-            nc.sync.dma_start(out=out[r0 : r0 + P, W * hb : W * hb + W], in_=res[:])
+            store(ua, fb, ub, res)
+
+        def finish_rows(ua, fb, ub):
+            mid[ua, fb, ub] = ring.tile([P, W], F32, name="mid", bufs=4)
+            nc.scalar.activation(out=mid[ua, fb, ub][:], in_=held["out", ua, fb, ub][:], func=ACT.Copy, scale=rsd[ua][:, fb : fb + 1])
+
+        def finish_columns(ua, fb, ub):
+            res = ring.tile([P, W], F32, name="res", bufs=6)
+            nc.gpsimd.tensor_tensor(out=res[:], in0=mid[ua, fb, ub][:], in1=rb[ub][:], op=ALU.mult)
+            store(ua, fb, ub, res)
+
+        jobs = []
+
+        def job(stage, engine, kind, length, after, emit, takes=None, frees=None):
+            jobs.append((stage, engine, kind, length, after, emit, takes, frees))
+            return len(jobs) - 1
+
+        def on_v(cols, count=1):
+            return cols + 36 * count
+
+        def on_s(cols, count=1):
+            return cols + 42 * count
+
+        TURN = 100
+        MULTIPLY = 534
+
+        weighted = job(-29, "V", "small", 420, [], weights)
+        counted = job(-18, "P", "sum", 180, [weighted], count, takes="n")
+        scaled = job(-18, "V", "small", 300, [counted], count_scale, frees="n")
+        widened, turned, quantised = [], [], []
+        for i in range(NT):
+            vec = "vsvvsvvv"[i] == "v"
+            widened.append(
+                job(-30 - 8 + i, "V" if vec else "S", "widen", on_v(D // 2, 8) if vec else on_s(D, 8), turned[i - 6 : i - 5] if i >= 6 else [], lambda i=i, vec=vec: widen(i, vec))
+            )
+            turned.append(job(-30 - 2 + i, "P", "turn", 516, [widened[i]], lambda bank, i=i: turn_x(i, bank), takes=("x", i)))
+            lifted = job(-30 - 2 + i, "S", "copy", on_s(W), [turned[i]] + (quantised[i - 6 : i - 5] if i >= 6 else []), lambda i=i: lift_x(i), frees=("x", i))
+            quantised.append(job(-30 - 2 + i, "V", "quantise", on_v(270), [lifted], lambda i=i: quantise_x(i)))
+
+        added = {}
+        ready = {}
+        coded = {}
+        squared = {}
+        stored = []
+        products = []
+        for u, (m, c0) in enumerate(GROUPS):
+            at = 10 * u
+            stored.append([])
+            for i in range(NT):
+                vec = u == 0 and i in (2, 5)
+                made = job(
+                    -30 + i if u == 0 else -10 + at, "P", "multiply", MULTIPLY, [quantised[i]] + ([stored[u - 1][i]] if u else []),
+                    lambda bank, u=u, i=i: multiply_x(u, i, bank), takes=("y", u, i),
+                )
+                stored[u].append(
+                    job(-30 + i if u == 0 else -10 + at, "V" if vec else "S", "relu", on_v(W) if vec else on_s(W) + 24, [made, weighted], lambda u=u, i=i, vec=vec: relu(u, i, vec), frees=("y", u, i))
+                )
+
+            folded = []
+            if u == 0:
+                half = NT // 2
+                last = {}
+                for i0 in (0, half):
+                    for fb in range(FB):
+                        def emit(bank, i0=i0, fb=fb):
+                            if i0 == 0:
+                                held["sum", 0, fb] = bank
+                            cols = slice(P * fb, P * fb + P)
+                            add_up(held["sum", 0, fb], slice(0, P), [th[0][:, i, cols] for i in range(i0, i0 + half)], i0 == 0, i0 == half)
+
+                        last[fb] = job(
+                            -30 + i0 + half + 4, "P", "turn", TURN * half, stored[0][i0 : i0 + half] + ([last[fb]] if i0 else []),
+                            emit, takes=("sum", 0, fb) if i0 == 0 else None,
+                        )
+                for fb in range(FB):
+                    folded.append(
+                        job(-8, "V", "fold", on_v(P), [last[fb]], lambda fb=fb: fold(sums[0][:, fb : fb + 1], held["sum", 0, fb], P), frees=("sum", 0, fb))
+                    )
+            else:
+                last = []
+                for fb in range(FB):
+                    def emit(bank, u=u, fb=fb):
+                        if fb == 0:
+                            held["sum", u] = bank
+                        cols = slice(P * fb, P * fb + P)
+                        add_up(held["sum", u], cols, [th[u][:, i, cols] for i in range(NT)])
+
+                    last.append(job(-8 + at, "P", "turn", TURN * NT, stored[u] + last, emit, takes=("sum", u) if fb == 0 else None))
+                folded.append(job(-8 + at, "V", "fold", on_v(W), last, lambda u=u: fold(sums[u][:], held["sum", u], W), frees=("sum", u)))
+
+            def emit(bank, u=u):
+                held["mean", u] = bank
+                spread(bank, sums[u])
+
+            known = job(-8 + at, "P", "turn", TURN * FB, folded, emit, takes=("mean", u))
+
+            centred = []
+            for i in range(NT):
+                centred.append(
+                    job(-1 + at, "V", "centre", on_v(W), [known, scaled], lambda u=u, i=i: centre(u, i), frees=("mean", u) if i == NT - 1 else None)
+                )
+            for g in range(G):
+                before = [coded[u - 2, g]] if u >= 2 else []
+                weighed = job(1 + at, "V", "weigh", on_v(W * T), centred[T * g : T * g + T] + before, lambda u=u, g=g: weigh(u, g))
+                coded[u, g] = job(5 + at, "V", "quantise", on_v(540), [weighed], lambda u=u, g=g: quantise_c(u, g))
+
+            squared[u] = []
+            for i in range(NT):
+                before = ([added[u - 2]] if u >= 2 else []) + squared[u][0:1]
+                squared[u].append(job(0 + at, "S", "square", on_s(W), [centred[i]] + before, lambda u=u, i=i: square(u, i)))
+            last = []
+            for fb in range(FB):
+                def emit(bank, u=u, fb=fb):
+                    if fb == 0:
+                        held["var", u] = bank
+                    cols = slice(P * fb, P * fb + P)
+                    add_up(held["var", u], cols, [sq[u][:, i, cols] for i in range(NT)])
+
+                last.append(job(12 + at, "P", "turn", TURN * NT, squared[u] + last, emit, takes=("var", u) if fb == 0 else None))
+            added[u] = last[-1]
+            summed = job(4 + at, "S", "fold", on_s(W + 260, FB), last, lambda u=u: fold_squares(u), frees=("var", u))
+            ready[u] = job(4 + at, "S", "small", on_s(4), [summed], lambda u=u: root(u))
+            if m == "b":
+                def emit(bank, u=u):
+                    held["rb", u] = bank
+                    spread(bank, rsd[u])
+
+                known = job(4 + at, "P", "turn", TURN * FB, [ready[u]], emit, takes=("rb", u))
+                ready[u] = job(4 + at, "S", "copy", on_s(W), [known], lambda u=u: nc.scalar.copy(out=rb[u][:], in_=held["rb", u][:]), frees=("rb", u))
+
+            products += [(v, u) if m == "b" else (u, v) for v in range(u) if GROUPS[v][0] != m]
+
+        for ua, ub in products:
+            for fb in range(FB):
+                at = 15 + 10 * max(ua, ub)
+                need = [coded[ua, g] for g in range(G)] + [coded[ub, g] for g in range(G)] + [ready[ua], ready[ub]]
+                made = job(at, "P", "multiply", MULTIPLY, need, lambda bank, k=(ua, fb, ub): multiply_c(*k, bank), takes=("out", ua, fb, ub))
+                if fb < {(1, 0): 4, (2, 0): 0, (1, 3): 0, (2, 3): 0}.get((ua, ub), 0):
+                    rows = job(at + 0, "S", "scale", on_s(W), [made], lambda k=(ua, fb, ub): finish_rows(*k), frees=("out", ua, fb, ub))
+                    job(0, "G", "scale", 2 * W + 420, [rows], lambda k=(ua, fb, ub): finish_columns(*k))
+                else:
+                    job(at, "V", "scale", on_v(W), [made], lambda k=(ua, fb, ub): finish(*k), frees=("out", ua, fb, ub))
 
         ctx.enter_context(tc.manual_schedule())
-
-        half = {}
-
-        def pair_add(j):
-            half[j] = ring.tile([P, W], F32, name="half", bufs=4)
-            nc.vector.tensor_tensor(out=half[j][:], in0=th[0][:, 2 * j, :], in1=th[0][:, 2 * j + 1, :], op=ALU.add)
-
-        for s in range(4 + 3):
-            if s < 4:
-                widen(2 * s, "v")
-                widen(2 * s + 1, "s")
-            if s == 0:
-                token_weights()
-            if 0 <= s - 1 < 4:
-                x_turn(2 * s - 2, 4)
-                x_turn(2 * s - 1, 5)
-                x_quant(2 * s - 2)
-                x_quant(2 * s - 1)
-            if 0 <= s - 2 < 4:
-                for i in (2 * s - 4, 2 * s - 3):
-                    relu(0, i, stage1(0, i, 6 + i % 2))
-            if 0 <= s - 3 < 4:
-                pair_add(s - 3)
-        z = bank(0)
-        for fb in range(4):
-            for j in range(4):
-                add_turned(z[:, P * fb : P * fb + P], half[j][:, P * fb : P * fb + P], j == 0, j == 3)
-        YB = [5, 6, 7]
-        n = 0
-        ys = {}
-        for i in range(2):
-            ys[i] = stage1(1, i, YB[n % 3])
-            n += 1
-        fold(vmean[0][:], z)
-        sums = spread(vmean[0], 4)
-        ys[2] = stage1(1, 2, YB[n % 3])
-        n += 1
-
-        SB = [4, 3, 4, 3]
-        for k in range(3):
-            for i in range(NT):
-                relu(k + 1, i, ys.pop(i))
-                if i + 3 < NT:
-                    ys[i + 3] = stage1(k + 1, i + 3, YB[n % 3])
-                    n += 1
-            for i in range(4):
-                centre(k, i, sums)
-            weigh(k, 0)
-            for i in range(4, 8):
-                centre(k, i, sums)
-            z = bank(0)
-            token_sum(th[k + 1], z)
-            if k < 2:
-                for i in range(3):
-                    ys[i] = stage1(k + 2, i, YB[n % 3])
-                    n += 1
-            weigh(k, 1)
-            fold(vmean[k + 1][:], z)
-            sums = spread(vmean[k + 1], SB[k + 1])
-            if k > 0:
-                zv = bank(1)
-                token_sum(sq[k - 1], zv)
-            for i in range(8):
-                square(k, i)
-            c_quant(k, 0)
-            c_quant(k, 1)
-            if k > 0:
-                fold(var[k - 1][:], zv)
-                inv_sd(k - 1)
-                if groups[k - 1][0] == "b":
-                    spread_b(k - 1, 2)
-            if k == 2:
-                held0 = [stage2(1, fb, 0, (1, 2, 5, 6)[fb]) for fb in range(4)]
-        k = 3
-        for i in range(4):
-            centre(k, i, sums)
-            square(k, i)
-        zv = bank(0)
-        token_sum(sq[2], zv)
-        weigh(k, 0)
-        for i in range(4, 8):
-            centre(k, i, sums)
-            square(k, i)
-        weigh(k, 1)
-        fold(var[2][:], zv)
-        inv_sd(2)
-        c_quant(k, 0)
-        finish(1, 0, 0, held0[0])
-        finish(1, 1, 0, held0[1])
-        c_quant(k, 1)
-        zq = [bank(b) for b in (4, 7, 0, 1)]
-        for fb in range(4):
-            for i in range(NT):
-                add_turned(zq[fb][:, 0:P], sq[3][:, i, P * fb : P * fb + P], i == 0, i == NT - 1)
-        finish(1, 2, 0, held0[2])
-        finish(1, 3, 0, held0[3])
-        for fb in range(4):
-            nc.vector.tensor_reduce(out=var[3][:, fb : fb + 1], in_=zq[fb][:, 0:P], axis=AX.X, op=ALU.add)
-        inv_sd(3)
-        for fb in range(4):
-            held0[fb] = stage2(2, fb, 0, (2, 5, 6, 3)[fb])
-        todo = [(ka, fb) for ka in (1, 2) for fb in range(4)]
-        banks = (7, 0, 1, 2, 5, 6, 3, 7)
-        held = {}
-        held[0] = stage2(todo[0][0], todo[0][1], 3, banks[0])
-        held[1] = stage2(todo[1][0], todo[1][1], 3, banks[1])
-        spread_b(3, 4)
-        for fb in range(4):
-            finish(2, fb, 0, held0[fb])
-        for n in range(8):
-            if n + 2 < 8:
-                held[n + 2] = stage2(todo[n + 2][0], todo[n + 2][1], 3, banks[n + 2])
-            finish(todo[n][0], todo[n][1], 3, held[n])
+        for j, b in plan(jobs):
+            emit, engine = jobs[j][5], jobs[j][1]
+            if engine == "P":
+                emit(psum.tile([P, W], F32, name="bank%d" % b) if b is not None else None)
+            else:
+                emit()

from contextlib import ExitStack

import concourse.mybir as mybir
from concourse.masks import make_identity

F32 = mybir.dt.float32
BF16 = mybir.dt.bfloat16
I32 = mybir.dt.int32
U32 = mybir.dt.uint32
U8 = mybir.dt.uint8
E4M3 = mybir.dt.float8_e4m3fn
E4M3X4 = mybir.dt.float8_e4m3fn_x4
E2M1X4 = mybir.dt.float4_e2m1fn_x4
ALU = mybir.AluOpType
ACT = mybir.ActivationFunctionType
AX = mybir.AxisListType

P = 128
T = 4
N = 1024
D = 1024
F = 1024
PASS = P * T
G = N // PASS
KG = D // PASS
NT = G * T
BLOCK = 128
W = 512
FB = W // P
BANKS = 8

GROUPS = (("b", 0), ("a", 0), ("a", W), ("b", W))
OWN = {"a": 0, "b": 1}
OUT_SCALE = 32.0

FLOPS = 2 * N * D * 2 * F + 2 * N * F * F


def plan(jobs):
    lag = 180
    free = {"V": 0.0, "S": 0.0, "P": 0.0, "G": 0.0}
    kinds = {e: "" for e in free}
    todo = {e: [j for j in range(len(jobs)) if jobs[j][1] == e] for e in free}
    ends = {}
    bank_free = {b: 0.0 for b in range(BANKS)}
    holds = {}
    order = []
    while len(order) < len(jobs):
        best = None
        for e in free:
            ready = []
            for j in todo[e]:
                stage, engine, kind, length, after, emit, takes, frees = jobs[j]
                if any(a not in ends for a in after) or (takes is not None and not bank_free):
                    continue
                begin = max([free[e]] + [ends[a] + (lag if jobs[a][1] != e else 0.0) for a in after])
                if takes is not None:
                    begin = max(begin, min(bank_free.values()) + lag)
                ready.append((begin, stage - (0.5 if kind == kinds[e] else 0.0), j))
            if ready:
                first = min(ready)[0]
                pick = min([(s, j) for begin, s, j in ready if begin <= first])[1]
                if best is None or first < best[0]:
                    best = (first, pick, e)
        begin, j, e = best
        stage, engine, kind, length, after, emit, takes, frees = jobs[j]
        kinds[e] = kind
        bank = None
        if takes is not None:
            bank = min(bank_free, key=lambda b: bank_free[b])
            holds[takes] = bank
            bank_free.pop(bank)
        ends[j] = free[e] = begin + length
        if frees is not None:
            bank_free[holds[frees]] = ends[j]
        todo[e].remove(j)
        order.append((j, bank))
    return order


def tile_zipitweightedfeaturecorrelation_d2p_kernel(tc, x_bytes, x_scale, wa_words, wa_scales, wb_words, wb_scales, p, q, out):
    nc = tc.nc
    with ExitStack() as ctx:
        keep = ctx.enter_context(tc.tile_pool(name="keep", bufs=1))
        ring = ctx.enter_context(tc.tile_pool(name="ring", bufs=2))
        psum = ctx.enter_context(tc.psum_pool(name="psum", bufs=1))

        xs_all = keep.tile([P, (N // BLOCK) * (D // BLOCK)], F32, name="xs_all")
        nc.scalar.dma_start(out=xs_all[:], in_=x_scale.rearrange("i j -> (i j)").partition_broadcast(P))
        weight16 = []
        for name, src in (("p16", p), ("q16", q)):
            weight16.append(keep.tile([P, G, T], BF16, name=name))
            nc.scalar.dma_start(out=weight16[-1][:], in_=src.rearrange("(g p t) -> p g t", p=P, t=T))

        x_view = x_bytes.rearrange("(g p t) k -> g p t k", p=P, t=T)
        xb = [keep.tile([P, T, D], U8, name="xb%d" % g) for g in range(G)]
        for g, t0, t1 in ((0, 0, 1), (0, 1, 2), (0, 2, 4), (1, 0, 4)):
            nc.sync.dma_start(out=xb[g][:, t0:t1, :], in_=x_view[g][:, t0:t1, :])

        ident = keep.tile([P, P], F32, name="ident")
        make_identity(nc, ident[:])
        ones = keep.tile([P, P], F32, name="ones")
        nc.gpsimd.memset(ones[:], 1.0)

        words, planes = {}, {}
        for m, w_scales in (("b", wb_scales), ("a", wa_scales)):
            words[m] = keep.tile([P, KG, 2 * F], U8, name="words_" + m, align_bytes=64)
            planes[m] = keep.tile([P, KG, F], U8, name="planes_" + m, align_bytes=64)
            nc.gpsimd.memset(planes[m][:].rearrange("p g n -> p (g n)").bitcast(I32), 0)
            src = w_scales.bitcast(I32).rearrange("g r n -> r g n")
            for r in range(4):
                nc.gpsimd.dma_start(out=planes[m][32 * r : 32 * r + 4].bitcast(I32), in_=src[4 * r : 4 * r + 4])
        for m, c0 in GROUPS:
            cols = slice(2 * c0, 2 * (c0 + W))
            w_words = wa_words if m == "a" else wb_words
            nc.sync.dma_start(out=words[m][:, :, cols].bitcast(I32), in_=w_words[:, :, cols].bitcast(I32).rearrange("g p n -> p g n"))

        xs = keep.tile([P, G, D // BLOCK], F32, name="xs")
        for r in range(4):
            rows = slice(32 * r, 32 * r + 32)
            nc.vector.tensor_copy(out=xs[rows], in_=xs_all[rows].rearrange("p (g r j) -> p r g j", g=G, r=4)[:, r])

        pq = keep.tile([P, 2, NT], F32, name="pq")
        rpq = keep.tile([P, 2, NT], F32, name="rpq")
        tw = keep.tile([P, NT], F32, name="tw")
        rst = keep.tile([P, NT], F32, name="rst")
        ntn = keep.tile([P, NT], F32, name="ntn")
        n_sum = keep.tile([P, 1], F32, name="n_sum")
        rn = keep.tile([P, 1], F32, name="rn")
        th = [keep.tile([P, NT, W], F32, name="th%d" % u) for u in range(len(GROUPS))]
        x_codes = [keep.tile([P, KG * P], U32, name="x_codes%d" % i, align_bytes=64) for i in range(NT)]
        x_plane = [keep.tile([P, KG * P], U8, name="x_plane%d" % i, align_bytes=64) for i in range(NT)]
        c_codes = [[keep.tile([P, W], U32, name="c_codes%d_%d" % (u, g), align_bytes=64) for g in range(G)] for u in range(len(GROUPS))]
        c_plane = [[keep.tile([P, W], U8, name="c_plane%d_%d" % (u, g), align_bytes=64) for g in range(G)] for u in range(len(GROUPS))]
        sums = [keep.tile([P, FB], F32, name="sums%d" % u) for u in range(len(GROUPS))]
        var = [keep.tile([P, FB], F32, name="var%d" % u) for u in range(len(GROUPS))]
        rsd = [keep.tile([P, FB], F32, name="rsd%d" % u) for u in range(len(GROUPS))]
        rb = {u: keep.tile([P, W], F32, name="rb%d" % u) for u in range(len(GROUPS)) if GROUPS[u][0] == "b"}

        held = {}
        xw, xg, pc, sq, mid = {}, {}, {}, {}, {}

        def turn(dst, src, first=True, last=True):
            nc.tensor.matmul(out=dst, lhsT=src, rhs=ident[:], start=first, stop=last, is_transpose=True)

        def add_up(bank, cols, tiles, at_start=True, at_end=True):
            for i, tile in enumerate(tiles):
                turn(bank[:, cols], tile, at_start and i == 0, at_end and i == len(tiles) - 1)

        def fold(dst, bank, width):
            nc.vector.tensor_reduce(out=dst, in_=bank[:, 0:width].rearrange("p (c r) -> p c r", r=P), axis=AX.X, op=ALU.add)

        def spread(bank, vec):
            for fb in range(FB):
                turn(bank[:, P * fb : P * fb + P], vec[:, fb : fb + 1].to_broadcast([P, P]))

        def weights():
            for own in range(2):
                nc.vector.tensor_copy(out=pq[:, own], in_=weight16[own][:].rearrange("p g t -> p (g t)"))
            nc.vector.tensor_tensor(out=tw[:], in0=pq[:, 0], in1=pq[:, 1], op=ALU.mult)
            nc.vector.reciprocal(out=rpq[:], in_=pq[:])
            nc.scalar.activation(out=rst[:], in_=tw[:], func=ACT.Abs_reciprocal_sqrt)

        def count(bank):
            held["n"] = bank
            nc.tensor.matmul(out=bank[:, 0:NT], lhsT=ones[:], rhs=tw[:], start=True, stop=True)

        def count_scale():
            nc.vector.tensor_reduce(out=n_sum[:], in_=held["n"][:, 0:NT], axis=AX.X, op=ALU.add)
            nc.vector.reciprocal(out=rn[:], in_=n_sum[:])
            nc.vector.tensor_scalar(out=ntn[:], in0=tw[:], scalar1=rn[:], scalar2=-1.0, op0=ALU.mult, op1=ALU.mult)

        def widen(i, on_vector):
            g, t = divmod(i, T)
            xw[i] = ring.tile([P, D], BF16, name="xw", bufs=6)
            for j in range(D // BLOCK):
                cols = slice(BLOCK * j, BLOCK * (j + 1))
                src, scale = xb[g][:, t, cols].bitcast(E4M3), xs[:, g, j : j + 1]
                if on_vector:
                    nc.vector.tensor_scalar(out=xw[i][:, cols], in0=src, scalar1=scale, scalar2=None, op0=ALU.mult)
                else:
                    nc.scalar.activation(out=xw[i][:, cols], in_=src, func=ACT.Copy, scale=scale)

        def turn_x(i, bank):
            held["x", i] = bank
            pairs = xw[i][:].bitcast(F32)
            for g in range(KG):
                for v in range(2):
                    turn(bank[:, P * (2 * g + v) : P * (2 * g + v + 1)], pairs[:, 256 * g + v : 256 * (g + 1) : 2])

        def lift_x(i):
            xg[i] = ring.tile([P, KG * P * T], BF16, name="xg", bufs=6, align_bytes=64)
            nc.scalar.copy(
                out=xg[i][:].bitcast(F32).rearrange("p (g r v) -> p g r v", g=KG, v=2),
                in_=held["x", i][:].rearrange("p (g v r) -> p g r v", g=KG, v=2),
            )

        def quantise_x(i):
            nc.vector.quantize_mx(out=x_codes[i][:].bitcast(E4M3X4), scales=x_plane[i][:], in_=xg[i][:])

        def multiply_x(u, i, bank):
            held["y", u, i] = bank
            m, c0 = GROUPS[u]
            for g in range(KG):
                nc.tensor.matmul_mx(
                    out=bank[:],
                    lhsT=x_codes[i][:, P * g : P * g + P].bitcast(E4M3X4),
                    lhsT_scale=x_plane[i][:, P * g : P * g + P],
                    rhs=words[m][:, g, 2 * c0 : 2 * (c0 + W)].bitcast(E2M1X4),
                    rhs_scale=planes[m][:, g, c0 : c0 + W],
                    start=(g == 0),
                    stop=(g == KG - 1),
                )

        def relu(u, i, on_vector):
            y, t = held["y", u, i], tw[:, i : i + 1]
            if on_vector:
                nc.vector.tensor_scalar(out=th[u][:, i, :], in0=y[:], scalar1=t, scalar2=0.0, op0=ALU.mult, op1=ALU.max)
            else:
                nc.scalar.activation(out=th[u][:, i, :], in_=y[:], func=ACT.Relu, scale=t)

        def centre(u, i):
            nc.vector.scalar_tensor_tensor(
                out=th[u][:, i, :], in0=held["mean", u][:], scalar=ntn[:, i : i + 1], in1=th[u][:, i, :], op0=ALU.mult, op1=ALU.add
            )

        def weigh(u, g):
            other = 1 - OWN[GROUPS[u][0]]
            pc[u, g] = ring.tile([P, W * T], BF16, name="pc", bufs=4, align_bytes=64)
            nc.vector.tensor_tensor(
                out=pc[u, g][:].rearrange("p (c i t) -> p c t i", i=4, t=T),
                in0=th[u][:, T * g : T * g + T, :].rearrange("p t (c i) -> p c t i", i=4),
                in1=rpq[:, other, T * g : T * g + T].unsqueeze(1).unsqueeze(3).to_broadcast([P, W // 4, T, 4]),
                op=ALU.mult,
            )

        def quantise_c(u, g):
            nc.vector.quantize_mx(out=c_codes[u][g][:].bitcast(E4M3X4), scales=c_plane[u][g][:], in_=pc[u, g][:])

        def square(u, i):
            if i == 0:
                sq[u] = ring.tile([P, NT, W], F32, name="sq", bufs=2)
            nc.scalar.activation(out=sq[u][:, i, :], in_=th[u][:, i, :], func=ACT.Square, scale=rst[:, i : i + 1])

        def fold_squares(u):
            scrap = ring.tile([P, W], F32, name="scrap", bufs=2)
            for fb in range(FB):
                cols = slice(P * fb, P * fb + P)
                nc.scalar.activation(out=scrap[:, cols], in_=held["var", u][:, cols], func=ACT.Copy, accum_out=var[u][:, fb : fb + 1])

        def root(u):
            unit = 1.0 / OUT_SCALE**2 if GROUPS[u][0] == "a" else 1.0
            nc.scalar.activation(out=rsd[u][:], in_=var[u][:], func=ACT.Abs_reciprocal_sqrt, scale=unit)

        def multiply_c(ua, fb, ub, bank):
            held["out", ua, fb, ub] = bank
            cols = slice(P * fb, P * fb + P)
            for g in range(G):
                nc.tensor.matmul_mx(
                    out=bank[:],
                    lhsT=c_codes[ua][g][:, cols].bitcast(E4M3X4),
                    lhsT_scale=c_plane[ua][g][:, cols],
                    rhs=c_codes[ub][g][:].bitcast(E4M3X4),
                    rhs_scale=c_plane[ub][g][:],
                    start=(g == 0),
                    stop=(g == G - 1),
                )

        def store(ua, fb, ub, tile):
            r0, c0 = GROUPS[ua][1] + P * fb, GROUPS[ub][1]
            nc.sync.dma_start(out=out[r0 : r0 + P, c0 : c0 + W], in_=tile[:])

        def finish(ua, fb, ub):
            res = ring.tile([P, W], F32, name="res", bufs=6)
            nc.vector.scalar_tensor_tensor(
                out=res[:], in0=held["out", ua, fb, ub][:], scalar=rsd[ua][:, fb : fb + 1], in1=rb[ub][:], op0=ALU.mult, op1=ALU.mult
            )
            store(ua, fb, ub, res)

        def finish_rows(ua, fb, ub):
            mid[ua, fb, ub] = ring.tile([P, W], F32, name="mid", bufs=4)
            nc.scalar.activation(out=mid[ua, fb, ub][:], in_=held["out", ua, fb, ub][:], func=ACT.Copy, scale=rsd[ua][:, fb : fb + 1])

        def finish_columns(ua, fb, ub):
            res = ring.tile([P, W], F32, name="res", bufs=6)
            nc.gpsimd.tensor_tensor(out=res[:], in0=mid[ua, fb, ub][:], in1=rb[ub][:], op=ALU.mult)
            store(ua, fb, ub, res)

        jobs = []

        def job(stage, engine, kind, length, after, emit, takes=None, frees=None):
            jobs.append((stage, engine, kind, length, after, emit, takes, frees))
            return len(jobs) - 1

        def on_v(cols, count=1):
            return cols + 36 * count

        def on_s(cols, count=1):
            return cols + 42 * count

        TURN = 100
        MULTIPLY = 534

        weighted = job(-29, "V", "small", 420, [], weights)
        counted = job(-18, "P", "sum", 180, [weighted], count, takes="n")
        scaled = job(-18, "V", "small", 300, [counted], count_scale, frees="n")
        widened, turned, quantised = [], [], []
        for i in range(NT):
            vec = "vsvvsvvv"[i] == "v"
            widened.append(
                job(-30 - 8 + i, "V" if vec else "S", "widen", on_v(D // 2, 8) if vec else on_s(D, 8), turned[i - 6 : i - 5] if i >= 6 else [], lambda i=i, vec=vec: widen(i, vec))
            )
            turned.append(job(-30 - 2 + i, "P", "turn", 516, [widened[i]], lambda bank, i=i: turn_x(i, bank), takes=("x", i)))
            lifted = job(-30 - 2 + i, "S", "copy", on_s(W), [turned[i]] + (quantised[i - 6 : i - 5] if i >= 6 else []), lambda i=i: lift_x(i), frees=("x", i))
            quantised.append(job(-30 - 2 + i, "V", "quantise", on_v(270), [lifted], lambda i=i: quantise_x(i)))

        added = {}
        ready = {}
        coded = {}
        squared = {}
        stored = []
        products = []
        for u, (m, c0) in enumerate(GROUPS):
            at = 10 * u
            stored.append([])
            for i in range(NT):
                vec = u == 0 and i in (2, 5)
                made = job(
                    -30 + i if u == 0 else -10 + at, "P", "multiply", MULTIPLY, [quantised[i]] + ([stored[u - 1][i]] if u else []),
                    lambda bank, u=u, i=i: multiply_x(u, i, bank), takes=("y", u, i),
                )
                stored[u].append(
                    job(-30 + i if u == 0 else -10 + at, "V" if vec else "S", "relu", on_v(W) if vec else on_s(W) + 24, [made, weighted], lambda u=u, i=i, vec=vec: relu(u, i, vec), frees=("y", u, i))
                )

            folded = []
            if u == 0:
                half = NT // 2
                last = {}
                for i0 in (0, half):
                    for fb in range(FB):
                        def emit(bank, i0=i0, fb=fb):
                            if i0 == 0:
                                held["sum", 0, fb] = bank
                            cols = slice(P * fb, P * fb + P)
                            add_up(held["sum", 0, fb], slice(0, P), [th[0][:, i, cols] for i in range(i0, i0 + half)], i0 == 0, i0 == half)

                        last[fb] = job(
                            -30 + i0 + half + 4, "P", "turn", TURN * half, stored[0][i0 : i0 + half] + ([last[fb]] if i0 else []),
                            emit, takes=("sum", 0, fb) if i0 == 0 else None,
                        )
                for fb in range(FB):
                    folded.append(
                        job(-8, "V", "fold", on_v(P), [last[fb]], lambda fb=fb: fold(sums[0][:, fb : fb + 1], held["sum", 0, fb], P), frees=("sum", 0, fb))
                    )
            else:
                last = []
                for fb in range(FB):
                    def emit(bank, u=u, fb=fb):
                        if fb == 0:
                            held["sum", u] = bank
                        cols = slice(P * fb, P * fb + P)
                        add_up(held["sum", u], cols, [th[u][:, i, cols] for i in range(NT)])

                    last.append(job(-8 + at, "P", "turn", TURN * NT, stored[u] + last, emit, takes=("sum", u) if fb == 0 else None))
                folded.append(job(-8 + at, "V", "fold", on_v(W), last, lambda u=u: fold(sums[u][:], held["sum", u], W), frees=("sum", u)))

            def emit(bank, u=u):
                held["mean", u] = bank
                spread(bank, sums[u])

            known = job(-8 + at, "P", "turn", TURN * FB, folded, emit, takes=("mean", u))

            centred = []
            for i in range(NT):
                centred.append(
                    job(-1 + at, "V", "centre", on_v(W), [known, scaled], lambda u=u, i=i: centre(u, i), frees=("mean", u) if i == NT - 1 else None)
                )
            for g in range(G):
                before = [coded[u - 2, g]] if u >= 2 else []
                weighed = job(1 + at, "V", "weigh", on_v(W * T), centred[T * g : T * g + T] + before, lambda u=u, g=g: weigh(u, g))
                coded[u, g] = job(5 + at, "V", "quantise", on_v(540), [weighed], lambda u=u, g=g: quantise_c(u, g))

            squared[u] = []
            for i in range(NT):
                before = ([added[u - 2]] if u >= 2 else []) + squared[u][0:1]
                squared[u].append(job(0 + at, "S", "square", on_s(W), [centred[i]] + before, lambda u=u, i=i: square(u, i)))
            last = []
            for fb in range(FB):
                def emit(bank, u=u, fb=fb):
                    if fb == 0:
                        held["var", u] = bank
                    cols = slice(P * fb, P * fb + P)
                    add_up(held["var", u], cols, [sq[u][:, i, cols] for i in range(NT)])

                last.append(job(12 + at, "P", "turn", TURN * NT, squared[u] + last, emit, takes=("var", u) if fb == 0 else None))
            added[u] = last[-1]
            summed = job(4 + at, "S", "fold", on_s(W + 260, FB), last, lambda u=u: fold_squares(u), frees=("var", u))
            ready[u] = job(4 + at, "S", "small", on_s(4), [summed], lambda u=u: root(u))
            if m == "b":
                def emit(bank, u=u):
                    held["rb", u] = bank
                    spread(bank, rsd[u])

                known = job(4 + at, "P", "turn", TURN * FB, [ready[u]], emit, takes=("rb", u))
                ready[u] = job(4 + at, "S", "copy", on_s(W), [known], lambda u=u: nc.scalar.copy(out=rb[u][:], in_=held["rb", u][:]), frees=("rb", u))

            products += [(v, u) if m == "b" else (u, v) for v in range(u) if GROUPS[v][0] != m]

        for ua, ub in products:
            for fb in range(FB):
                at = 15 + 10 * max(ua, ub)
                need = [coded[ua, g] for g in range(G)] + [coded[ub, g] for g in range(G)] + [ready[ua], ready[ub]]
                made = job(at, "P", "multiply", MULTIPLY, need, lambda bank, k=(ua, fb, ub): multiply_c(*k, bank), takes=("out", ua, fb, ub))
                if fb < {(1, 0): 4, (2, 0): 0, (1, 3): 0, (2, 3): 0}.get((ua, ub), 0):
                    rows = job(at + 0, "S", "scale", on_s(W), [made], lambda k=(ua, fb, ub): finish_rows(*k), frees=("out", ua, fb, ub))
                    job(0, "G", "scale", 2 * W + 420, [rows], lambda k=(ua, fb, ub): finish_columns(*k))
                else:
                    job(at, "V", "scale", on_v(W), [made], lambda k=(ua, fb, ub): finish(*k), frees=("out", ua, fb, ub))

        ctx.enter_context(tc.manual_schedule())
        for j, b in plan(jobs):
            emit, engine = jobs[j][5], jobs[j][1]
            if engine == "P":
                emit(psum.tile([P, W], F32, name="bank%d" % b) if b is not None else None)
            else:
                emit()
